import numpy as np
import ml_dtypes


def mxq(x, axis, fmt="e4m3"):
    dtype, down = {"e4m3": (ml_dtypes.float8_e4m3fn, 7), "e5m2": (ml_dtypes.float8_e5m2, 14)}[fmt]
    v = np.moveaxis(np.asarray(x, np.float32).astype(ml_dtypes.bfloat16).astype(np.float64), axis, -1)
    blocks = v.reshape(v.shape[:-1] + (-1, 32))
    amax = np.abs(blocks).max(-1, keepdims=True)
    byte = np.maximum(np.where(amax > 0, np.frexp(amax)[1] - 1 + 127, 0) - down, 1)
    scale = np.exp2(byte - 127.0)
    codes = (blocks / scale).astype(np.float32).astype(dtype).astype(np.float64)
    return np.moveaxis((codes * scale).reshape(v.shape), -1, axis)


WIDE = False


def mx_kscale(k):
    if not WIDE:
        return np.ones(k)
    levels = np.array([10, -10, 5, -5, 0])
    if k % 512:
        return np.exp2(np.random.permutation(np.resize(levels, k // 32))).repeat(32)
    a = np.empty((k // 512, 16))
    for p in range(k // 512):
        a[p, :8] = np.random.permutation(np.resize(levels, 8))
        for g in range(8):
            far = levels[np.abs(levels - a[p, g]) >= 10]
            a[p, g + 8] = far[np.random.randint(len(far))]
    return np.exp2(a.ravel()).repeat(32)


def f64(x):
    return np.asarray(x).astype(np.float64)


def striped(idx):
    return np.tile(np.asarray(idx).reshape(-1, 16).T, (8, 1)).astype(np.uint16)


def unstriped(offs):
    return offs[:16].T.reshape(-1).astype(np.int64)


def striped8(idx):
    return np.asarray(idx).reshape(8, -1, 16).transpose(0, 2, 1).reshape(128, -1).astype(np.uint16)


def unstriped8(offs):
    return offs.reshape(8, 16, -1).transpose(0, 2, 1).reshape(8, -1).astype(np.int64)


def pick8(x, idx, run):
    r = np.arange(len(x))
    return x[r[:, None], idx[r % (8 * run) // run]]


E2M1 = np.array([0.0, 0.5, 1.0, 1.5, 2.0, 3.0, 4.0, 6.0, -0.0, -0.5, -1.0, -1.5, -2.0, -3.0, -4.0, -6.0])


def pack_weight(w, fmt):
    k, n = w.shape
    w = f64(np.asarray(w, np.float32).astype(ml_dtypes.bfloat16)).reshape(k // 32, 32, n)
    amax = np.abs(w).max(1)
    if fmt == "e4m3":
        byte = np.frexp(amax)[1] - 1 + 127 - 7
    else:
        mant, ex = np.frexp(amax / 6.0)
        byte = np.where(mant > 0.5, ex, ex - 1) + 127
    byte = np.clip(np.where(amax > 0, byte, 1), 1, 254)
    scaled = (w * np.exp2(127.0 - byte)[:, None, :]).reshape(k, n).astype(np.float32)
    by_word = np.ascontiguousarray(scaled.reshape(k // 512, 128, 4, n).transpose(0, 1, 3, 2))
    if fmt == "e4m3":
        words = by_word.astype(ml_dtypes.float8_e4m3fn).view(np.uint8)
    else:
        c = by_word.astype(ml_dtypes.float4_e2m1fn).view(np.uint8) & 0xF
        words = (c[..., 0::2] | (c[..., 1::2] << 4)).reshape(k // 512, 128, 2 * n)
    return np.ascontiguousarray(words), np.ascontiguousarray(byte.astype(np.uint8).reshape(k // 512, 16, n))


def unpack_weight(words, scales, fmt):
    g, _, n = scales.shape
    words = np.ascontiguousarray(words).reshape(g, 128, n, -1)
    if fmt == "e4m3":
        vals = words.view(ml_dtypes.float8_e4m3fn).astype(np.float64)
    else:
        nib = np.empty((g, 128, n, 4), np.uint8)
        nib[..., 0::2] = words & 0xF
        nib[..., 1::2] = words >> 4
        vals = E2M1[nib]
    vals = vals * np.repeat(np.exp2(scales.astype(np.float64) - 127.0), 8, axis=1)[..., None]
    return vals.transpose(0, 1, 3, 2).reshape(g * 512, n)


K, J, R, T, F, Z, M, O, C, N = 512, 512, 512, 1024, 1024, 512, 1024, 256, 1024, 256


def setup_inputs():
    n = np.random.standard_normal
    idx = np.stack([np.random.permutation(T)[:J] for _ in range(8)])
    idx2 = np.stack([np.random.permutation(F)[:R] for _ in range(8)])
    idx3 = np.stack([np.random.permutation(F)[:R] for _ in range(8)])
    idx4 = np.random.permutation(M)[:J]
    idx5 = np.stack([np.random.permutation(C)[:J] for _ in range(8)])
    idx6 = np.stack([np.random.permutation(C)[:O] for _ in range(8)])
    idx7 = np.stack([np.random.permutation(J)[:O] for _ in range(8)])
    fk = mx_kscale(K)
    fz = mx_kscale(Z)
    fr = mx_kscale(R)
    xop = pack_weight(n((Z, M)) / fz[:, None], "e4m3")
    w2p = pack_weight(n((Z, R)) * 1 / np.sqrt(Z) * fz[:, None], "e2m1")
    wbp = pack_weight(n((R, N)) * 1 / np.sqrt(R) / fr[:, None], "e2m1")
    return {
        "ta": (np.random.randint(-7, 8, (K, T)).astype(np.float64)).astype(np.float32),
        "ga": ((np.random.randint(8, 25, (K, 1)) / 64.0) * fk[:, None]).astype(np.float32),
        "ua": (np.random.randint(-7, 8, (K, F)).astype(np.float64)).astype(np.float32),
        "ha": ((np.random.randint(10, 25, (K, 1)) / 1024.0) / fk[:, None]).astype(np.float32),
        "hb": ((np.random.randint(4, 13, (K, 1)) / 1024.0) / fk[:, None]).astype(np.float32),
        "xo_words": xop[0],
        "xo_scales": xop[1],
        "w2_words": w2p[0],
        "w2_scales": w2p[1],
        "sa": (np.random.uniform(0.5, 1.6, (R, 1)) * fr[:, None]).astype(np.float32),
        "sb": (np.random.uniform(0.5, 1.6, (R, 1)) * fr[:, None]).astype(np.float32),
        "wb_words": wbp[0],
        "wb_scales": wbp[1],
        "offs": striped8(idx),
        "offs2": striped8(idx2),
        "offs3": striped8(idx3),
        "offs4": striped(idx4),
        "offs5": striped8(idx5),
        "offs6": striped8(idx6),
        "offs7": striped8(idx7),
    }


def reference(ta, ga, ua, ha, hb, xo_words, xo_scales, w2_words, w2_scales, sa, sb, wb_words, wb_scales, offs, offs2, offs3, offs4, offs5, offs6, offs7):
    idx = unstriped8(offs)
    idx2 = unstriped8(offs2)
    idx3 = unstriped8(offs3)
    idx4 = unstriped(offs4)
    idx5 = unstriped8(offs5)
    idx6 = unstriped8(offs6)
    idx7 = unstriped8(offs7)
    xou = unpack_weight(xo_words, xo_scales, "e4m3")
    w2u = unpack_weight(w2_words, w2_scales, "e2m1")
    wbu = unpack_weight(wb_words, wb_scales, "e2m1")
    xc = pick8(f64(ta), idx, 64) * f64(ga)
    wc = pick8(f64(ua), idx2, 64) * f64(ha) + pick8(f64(ua), idx3, 64) * f64(hb)
    wcq = mxq(wc, 0, "e4m3")
    xcq = mxq(xc, 0, "e4m3")
    a = wcq.T @ xcq
    xoidx4g = xou[:, idx4]
    b = w2u.T @ xoidx4g
    pw = np.zeros((R, C))
    pw[np.arange(R)[:, None], idx5[np.arange(R) % 512 // 64]] = a
    hid = np.maximum(pick8(pw, idx6, 64) * f64(sa), pick8(b, idx7, 64) * f64(sb))
    hidq = mxq(hid, 0, "e4m3")
    y = wbu.T @ hidq
    return y

@@ -1,0 +1,284 @@
+from contextlib import ExitStack
+
+import concourse.mybir as mybir
+
+K, J, R, T, F, Z, M, O, C, N = 512, 512, 512, 1024, 1024, 512, 1024, 256, 1024, 256
+FLOPS = 2 * (K * R * J + Z * R * J + R * N * O)
+
+F32 = mybir.dt.float32
+BF16 = mybir.dt.bfloat16
+I32 = mybir.dt.int32
+U32 = mybir.dt.uint32
+U16 = mybir.dt.uint16
+U8 = mybir.dt.uint8
+FP8X4 = mybir.dt.float8_e4m3fn_x4
+FP4X4 = mybir.dt.float4_e2m1fn_x4
+COPY = mybir.ActivationFunctionType.Copy
+ADD = mybir.AluOpType.add
+MAX = mybir.AluOpType.max
+
+P = 128
+PACK = 4
+HALF = J // 2
+STRIPE = 16
+RUN = 4
+
+
+def tile_picked_codes_refined_two_boardmeet_one_plain_kernel(
+    tc, ta, ga, ua, ha, hb, xo_words, xo_scales, w2_words, w2_scales, sa, sb, wb_words, wb_scales,
+    offs, offs2, offs3, offs4, offs5, offs6, offs7, out,
+):
+    nc = tc.nc
+    with ExitStack() as ctx:
+        keep = ctx.enter_context(tc.tile_pool(name="keep", bufs=1))
+        psum = ctx.enter_context(tc.psum_pool(name="psum", bufs=1))
+
+        def new(shape, dtype, name):
+            return keep.tile(shape, dtype, name=name, align_bytes=64)
+
+        def load_list(src, name):
+            dst = keep.tile(list(src.shape), U16, name=name)
+            nc.sync.dma_start(dst[:], src)
+            return dst
+
+        def load_factor(queue, src, name):
+            dst = new([P, PACK], F32, name)
+            queue.dma_start(dst[:], src.rearrange("(p t) one -> p (t one)", t=PACK))
+            return dst
+
+        def load_plane(src, t, name):
+            dst = new([P, src.shape[1]], F32, name)
+            nc.sync.dma_start(dst[:], src.rearrange("(p t) c -> p t c", t=PACK)[:, t, :])
+            return dst
+
+        def load_words(src, dtype, width, name):
+            dst = new([P, width], dtype, name)
+            nc.sync.dma_start(dst[:].bitcast(I32), src.bitcast(I32))
+            return dst
+
+        def load_scale_rows(src, name):
+            width = src.shape[2]
+            stage = new([4, 4, width // 4], I32, name)
+            nc.sync.dma_start(stage[:], src[0].bitcast(I32).rearrange("(q i) w -> i q w", i=4))
+            return stage
+
+        def zeroed_plane(width, name):
+            plane = new([P, width], U8, name)
+            nc.vector.memset(plane[:].bitcast(I32), 0)
+            return plane
+
+        def spread(plane, stage):
+            for q in range(4):
+                nc.vector.tensor_copy(out=plane[32 * q : 32 * q + 4, :].bitcast(I32), in_=stage[:, q, :])
+
+        def interleave(engine_copy, dst, src):
+            engine_copy(
+                out=dst.rearrange("p (c i) t -> p c t i", i=RUN),
+                in_=src.rearrange("p t (c i) -> p c t i", i=RUN),
+            )
+
+        def quantize(codes, scales, grouped):
+            nc.vector.quantize_mx(out=codes.bitcast(FP8X4), scales=scales, in_=grouped.rearrange("p c t -> p (c t)"))
+
+        l2 = load_list(offs2, "l2")
+        ha_sb = load_factor(nc.scalar, ha, "ha_sb")
+        hb_sb = load_factor(nc.scalar, hb, "hb_sb")
+        ua_sb = [load_plane(ua, 0, "ua0")]
+        l3 = load_list(offs3, "l3")
+        xs_stage = load_scale_rows(xo_scales, "xs_stage")
+        l4 = load_list(offs4, "l4")
+        xo_sb = load_words(xo_words[0].rearrange("p c t -> p (c t)"), U32, M, "xo_sb")
+        w2s_stage = load_scale_rows(w2_scales, "w2s_stage")
+        w2_raw = load_words(w2_words[0], U8, 2 * R, "w2_raw")
+        ua_sb.append(load_plane(ua, 1, "ua1"))
+        ua_sb.append(load_plane(ua, 2, "ua2"))
+        ua_sb.append(load_plane(ua, 3, "ua3"))
+        l1 = load_list(offs, "l1")
+        ga_sb = load_factor(nc.sync, ga, "ga_sb")
+        ta_sb = [load_plane(ta, t, "ta%d" % t) for t in range(PACK)]
+        l5 = load_list(offs5, "l5")
+        l7 = load_list(offs7, "l7")
+        sb_sb = load_factor(nc.sync, sb, "sb_sb")
+        l6 = load_list(offs6, "l6")
+        sa_sb = load_factor(nc.sync, sa, "sa_sb")
+        wb_sb = load_words(wb_words[0], U8, 2 * N, "wb_sb")
+
+        xs_plane = zeroed_plane(M, "xs_plane")
+        w2s_plane = zeroed_plane(R, "w2s_plane")
+        wbs_plane = zeroed_plane(N, "wbs_plane")
+        for q in range(4):
+            nc.sync.dma_start(
+                wbs_plane[32 * q : 32 * q + 4, :].bitcast(I32), wb_scales[0, 4 * q : 4 * q + 4, :].bitcast(I32)
+            )
+        board = [new([P, C], F32, "board%d" % t) for t in range(PACK)]
+        for t in range(PACK):
+            (nc.vector if t < 2 else nc.gpsimd).memset(board[t][:], 0.0)
+
+        wc_pairs = new([P, 2, R, 2], BF16, "wc_pairs")
+
+        def wc_plane(t):
+            coarse = new([P, R], F32, "coarse%d" % t)
+            fine = new([P, R], F32, "fine%d" % t)
+            nc.scalar.activation(out=coarse[:], in_=ua_sb[t][:].indirect(l2[:]), func=COPY, scale=ha_sb[:, t : t + 1])
+            nc.scalar.activation(out=fine[:], in_=ua_sb[t][:].indirect(l3[:]), func=COPY, scale=hb_sb[:, t : t + 1])
+            nc.vector.tensor_tensor(
+                out=wc_pairs[:, t // 2, :, t % 2].rearrange("p (u m) -> p m u", u=PACK),
+                in0=coarse[:].rearrange("p (m u) -> p m u", u=PACK),
+                in1=fine[:].rearrange("p (m u) -> p m u", u=PACK),
+                op=ADD,
+            )
+
+        spread(xs_plane, xs_stage)
+        note_codes = new([P, J], U32, "note_codes")
+        note_sc = new([P, J], U8, "note_sc")
+        nc.vector.tensor_copy(out=note_sc[:], in_=xs_plane[:].indirect(l4[:]))
+        nc.vector.tensor_copy(out=note_codes[:], in_=xo_sb[:].indirect(l4[:]))
+        spread(w2s_plane, w2s_stage)
+        w2_codes = new([P, 2 * R], U8, "w2_codes")
+        w2_sc = new([P, R], U8, "w2_sc")
+        nc.vector.tensor_copy(
+            out=w2_codes[:].bitcast(U16).rearrange("p (u m) -> p m u", u=PACK),
+            in_=w2_raw[:].bitcast(U16).rearrange("p (m u) -> p m u", u=PACK),
+        )
+        nc.vector.tensor_copy(
+            out=w2_sc[:].rearrange("p (u m) -> p m u", u=PACK),
+            in_=w2s_plane[:].rearrange("p (m u) -> p m u", u=PACK),
+        )
+        b_sb, b_banks = [], []
+        for u in range(PACK):
+            bank = psum.tile([P, J], F32, name="b_bank%d" % u)
+            nc.tensor.matmul_mx(
+                out=bank[:],
+                lhsT=w2_codes[:, 2 * P * u : 2 * P * (u + 1)].bitcast(FP4X4),
+                lhsT_scale=w2_sc[:, P * u : P * (u + 1)],
+                rhs=note_codes[:].bitcast(FP8X4),
+                rhs_scale=note_sc[:],
+                start=True,
+                stop=True,
+            )
+            b_banks.append(bank)
+
+        def b_rows(u, copy_out, tag):
+            rows = new([P, J], F32, tag)
+            copy_out(out=rows[:], in_=b_banks[u][:])
+            b_sb.append(rows)
+
+        for u in range(2):
+            b_rows(u, nc.vector.tensor_copy, "b%d" % u)
+
+        for t in range(PACK):
+            wc_plane(t)
+        wc_grouped = new([P, R, PACK], BF16, "wc_grouped")
+        nc.vector.tensor_copy(
+            out=wc_grouped[:].bitcast(F32).rearrange("p (c i) g -> p c g i", i=RUN),
+            in_=wc_pairs[:].bitcast(F32).rearrange("p g (c i) one -> p c g (i one)", i=RUN),
+        )
+        wc_codes, wc_sc = [], []
+
+        def wc_quantize(v, tag):
+            codes = new([P, 2 * P], U32, tag)
+            scales = new([P, 2 * P], U8, "wc_sc%d" % v)
+            quantize(codes[:], scales[:], wc_grouped[:, 2 * P * v : 2 * P * (v + 1), :])
+            wc_codes.append(codes)
+            wc_sc.append(scales)
+
+        wc_quantize(0, "wc_codes0")
+
+        def xc_gather(h, tag):
+            planes = new([P, PACK, HALF], BF16, tag)
+            cols = slice(h * HALF // STRIPE, (h + 1) * HALF // STRIPE)
+            for t in range(PACK):
+                nc.scalar.activation(
+                    out=planes[:, t, :], in_=ta_sb[t][:].indirect(l1[:, cols]), func=COPY, scale=ga_sb[:, t : t + 1]
+                )
+            return planes
+
+        def a_piece(u, codes, scales, bank_tag, rows_tag):
+            width = codes.shape[1]
+            bank = psum.tile([P, width], F32, name=bank_tag)
+            nc.tensor.matmul_mx(
+                out=bank[:],
+                lhsT=wc_codes[u // 2][:, P * (u % 2) : P * (u % 2 + 1)].bitcast(FP8X4),
+                lhsT_scale=wc_sc[u // 2][:, P * (u % 2) : P * (u % 2 + 1)],
+                rhs=codes.bitcast(FP8X4),
+                rhs_scale=scales,
+                start=True,
+                stop=True,
+            )
+            rows = new([P, width], F32, rows_tag)
+            nc.scalar.copy(out=rows[:], in_=bank[:])
+            return rows
+
+        def scatter(u, first, rows):
+            width = rows.shape[1]
+            nc.vector.tensor_copy(
+                out=board[u][:].indirect(l5[:, first // STRIPE : (first + width) // STRIPE]), in_=rows[:]
+            )
+
+        planes0 = xc_gather(0, "xc_planes0")
+        grouped0 = [new([P, P, PACK], BF16, "xc_grouped0_%d" % s) for s in range(2)]
+        codes0 = new([P, HALF], U32, "xc_codes0")
+        sc0 = new([P, HALF], U8, "xc_sc0")
+        for s in range(2):
+            interleave(nc.vector.tensor_copy, grouped0[s][:], planes0[:, :, P * s : P * (s + 1)])
+        for s in range(2):
+            quantize(codes0[:, P * s : P * (s + 1)], sc0[:, P * s : P * (s + 1)], grouped0[s][:])
+        wc_quantize(1, "xc_planes0")
+        first = [
+            a_piece(0, codes0[:, P * s : P * (s + 1)], sc0[:, P * s : P * (s + 1)], "a_bank%d" % s, "a0_0_%d" % s)
+            for s in range(2)
+        ]
+        rows0 = [a_piece(u, codes0[:], sc0[:], ("b_bank0", "b_bank1", "a_bank2")[u - 1], "a%d_0" % u) for u in range(1, PACK)]
+        for s in range(2):
+            scatter(0, P * s, first[s])
+        for u in range(1, PACK):
+            scatter(u, 0, rows0[u - 1])
+
+        planes1 = xc_gather(1, "xc_codes0")
+        grouped1 = new([P, HALF, PACK], BF16, "xc_grouped1")
+        interleave(nc.scalar.copy, grouped1[:], planes1[:])
+        b_rows(2, nc.scalar.copy, "a1_0")
+        b_rows(3, nc.scalar.copy, "xc_codes0")
+        codes1 = new([P, HALF], U32, "a2_0")
+        sc1 = new([P, HALF], U8, "xc_sc1")
+        quantize(codes1[:], sc1[:], grouped1[:])
+        rows1 = [a_piece(u, codes1[:], sc1[:], ("a_bank3", "a_bank0", "a_bank1", "a_bank2")[u], "a%d_1" % u) for u in range(PACK)]
+        for u in range(PACK):
+            scatter(u, HALF, rows1[u])
+
+        from_board = new([P, PACK, O], F32, "from_board")
+        from_b = new([P, PACK, O], F32, "a2_0")
+        for u in range(PACK):
+            nc.scalar.activation(
+                out=from_b[:, u, :], in_=b_sb[u][:].indirect(l7[:]), func=COPY, scale=sb_sb[:, u : u + 1]
+            )
+        for u in range(PACK):
+            nc.scalar.activation(
+                out=from_board[:, u, :], in_=board[u][:].indirect(l6[:]), func=COPY, scale=sa_sb[:, u : u + 1]
+            )
+
+        hid = new([P, O, PACK], BF16, "hid")
+        for rows in (slice(0, PACK - 1), slice(PACK - 1, PACK)):
+            nc.vector.tensor_tensor(
+                out=hid[:, :, rows].rearrange("p (c i) t -> p c t i", i=RUN),
+                in0=from_board[:, rows, :].rearrange("p t (c i) -> p c t i", i=RUN),
+                in1=from_b[:, rows, :].rearrange("p t (c i) -> p c t i", i=RUN),
+                op=MAX,
+            )
+        hid_codes = new([P, O], U32, "hid_codes")
+        hid_sc = new([P, O], U8, "hid_sc")
+        quantize(hid_codes[:], hid_sc[:], hid[:])
+        for v, (copy_out, queue) in enumerate(((nc.vector.tensor_copy, nc.sync), (nc.scalar.copy, nc.scalar))):
+            bank = psum.tile([P, O], F32, name="b_bank%d" % v)
+            nc.tensor.matmul_mx(
+                out=bank[:],
+                lhsT=wb_sb[:, 2 * P * v : 2 * P * (v + 1)].bitcast(FP4X4),
+                lhsT_scale=wbs_plane[:, P * v : P * (v + 1)],
+                rhs=hid_codes[:].bitcast(FP8X4),
+                rhs_scale=hid_sc[:],
+                start=True,
+                stop=True,
+            )
+            result = new([P, O], F32, "result%d" % v)
+            copy_out(out=result[:], in_=bank[:])
+            queue.dma_start(out[P * v : P * (v + 1), :], result[:])

@@ -103,6 +103,11 @@ def tile_picked_codes_refined_two_boardmeet_one_plain_kernel(
         sa_sb = load_factor(nc.sync, sa, "sa_sb")
         wb_sb = load_words(wb_words[0], U8, 2 * N, "wb_sb")
 
+        warm_in = new([P, 1], F32, "warm_in")
+        warm_out = new([P, 1], F32, "warm_out")
+        nc.gpsimd.memset(warm_in[:], 0.0)
+        nc.scalar.activation(out=warm_out[:], in_=warm_in[:], func=COPY)
+
         xs_plane = zeroed_plane(M, "xs_plane")
         w2s_plane = zeroed_plane(R, "w2s_plane")
         wbs_plane = zeroed_plane(N, "wbs_plane")

@@ -62,9 +62,9 @@ def tile_picked_codes_refined_two_boardmeet_one_plain_kernel(
             nc.sync.dma_start(stage[:], src[0].bitcast(I32).rearrange("(q i) w -> i q w", i=4))
             return stage
 
-        def zeroed_plane(width, name):
+        def zeroed_plane(engine, width, name):
             plane = new([P, width], U8, name)
-            nc.vector.memset(plane[:].bitcast(I32), 0)
+            engine.memset(plane[:].bitcast(I32), 0)
             return plane
 
         def spread(plane, stage):
@@ -80,17 +80,27 @@ def tile_picked_codes_refined_two_boardmeet_one_plain_kernel(
         def quantize(codes, scales, grouped):
             nc.vector.quantize_mx(out=codes.bitcast(FP8X4), scales=scales, in_=grouped.rearrange("p c t -> p (c t)"))
 
+        xs_plane = zeroed_plane(nc.gpsimd, M, "xs_plane")
+        w2s_plane = zeroed_plane(nc.vector, R, "w2s_plane")
+        wbs_plane = zeroed_plane(nc.vector, N, "wbs_plane")
+
+        def load_scales_in_place(plane, src):
+            for q in range(4):
+                nc.sync.dma_start(
+                    plane[32 * q : 32 * q + 4, :].bitcast(I32), src[0, 4 * q : 4 * q + 4, :].bitcast(I32)
+                )
+
         l2 = load_list(offs2, "l2")
         ha_sb = load_factor(nc.scalar, ha, "ha_sb")
         hb_sb = load_factor(nc.scalar, hb, "hb_sb")
         ua_sb = [load_plane(ua, 0, "ua0")]
         l3 = load_list(offs3, "l3")
-        xs_stage = load_scale_rows(xo_scales, "xs_stage")
+        w2s_stage = load_scale_rows(w2_scales, "w2s_stage")
+        ua_sb.append(load_plane(ua, 1, "ua1"))
         l4 = load_list(offs4, "l4")
         xo_sb = load_words(xo_words[0].rearrange("p c t -> p (c t)"), U32, M, "xo_sb")
-        w2s_stage = load_scale_rows(w2_scales, "w2s_stage")
+        load_scales_in_place(xs_plane, xo_scales)
         w2_raw = load_words(w2_words[0], U8, 2 * R, "w2_raw")
-        ua_sb.append(load_plane(ua, 1, "ua1"))
         ua_sb.append(load_plane(ua, 2, "ua2"))
         ua_sb.append(load_plane(ua, 3, "ua3"))
         l1 = load_list(offs, "l1")
@@ -103,51 +113,31 @@ def tile_picked_codes_refined_two_boardmeet_one_plain_kernel(
         sa_sb = load_factor(nc.sync, sa, "sa_sb")
         wb_sb = load_words(wb_words[0], U8, 2 * N, "wb_sb")
 
+        load_scales_in_place(wbs_plane, wb_scales)
+
         warm_in = new([P, 1], F32, "warm_in")
         warm_out = new([P, 1], F32, "warm_out")
         nc.gpsimd.memset(warm_in[:], 0.0)
         nc.scalar.activation(out=warm_out[:], in_=warm_in[:], func=COPY)
 
-        xs_plane = zeroed_plane(M, "xs_plane")
-        w2s_plane = zeroed_plane(R, "w2s_plane")
-        wbs_plane = zeroed_plane(N, "wbs_plane")
-        for q in range(4):
-            nc.sync.dma_start(
-                wbs_plane[32 * q : 32 * q + 4, :].bitcast(I32), wb_scales[0, 4 * q : 4 * q + 4, :].bitcast(I32)
-            )
         board = [new([P, C], F32, "board%d" % t) for t in range(PACK)]
         for t in range(PACK):
             (nc.vector if t < 2 else nc.gpsimd).memset(board[t][:], 0.0)
 
-        wc_pairs = new([P, 2, R, 2], BF16, "wc_pairs")
-
-        def wc_plane(t):
-            coarse = new([P, R], F32, "coarse%d" % t)
-            fine = new([P, R], F32, "fine%d" % t)
-            nc.scalar.activation(out=coarse[:], in_=ua_sb[t][:].indirect(l2[:]), func=COPY, scale=ha_sb[:, t : t + 1])
-            nc.scalar.activation(out=fine[:], in_=ua_sb[t][:].indirect(l3[:]), func=COPY, scale=hb_sb[:, t : t + 1])
-            nc.vector.tensor_tensor(
-                out=wc_pairs[:, t // 2, :, t % 2].rearrange("p (u m) -> p m u", u=PACK),
-                in0=coarse[:].rearrange("p (m u) -> p m u", u=PACK),
-                in1=fine[:].rearrange("p (m u) -> p m u", u=PACK),
-                op=ADD,
-            )
-
-        spread(xs_plane, xs_stage)
-        note_codes = new([P, J], U32, "note_codes")
-        note_sc = new([P, J], U8, "note_sc")
-        nc.vector.tensor_copy(out=note_sc[:], in_=xs_plane[:].indirect(l4[:]))
-        nc.vector.tensor_copy(out=note_codes[:], in_=xo_sb[:].indirect(l4[:]))
         spread(w2s_plane, w2s_stage)
         w2_codes = new([P, 2 * R], U8, "w2_codes")
         w2_sc = new([P, R], U8, "w2_sc")
         nc.vector.tensor_copy(
-            out=w2_codes[:].bitcast(U16).rearrange("p (u m) -> p m u", u=PACK),
-            in_=w2_raw[:].bitcast(U16).rearrange("p (m u) -> p m u", u=PACK),
+            out=w2_sc[:].rearrange("p (u m) -> p u m", u=PACK),
+            in_=w2s_plane[:].rearrange("p (m u) -> p u m", u=PACK),
         )
+        note_codes = new([P, J], U32, "note_codes")
+        note_sc = new([P, J], U8, "note_sc")
+        nc.vector.tensor_copy(out=note_codes[:], in_=xo_sb[:].indirect(l4[:]))
+        nc.vector.tensor_copy(out=note_sc[:], in_=xs_plane[:].indirect(l4[:]))
         nc.vector.tensor_copy(
-            out=w2_sc[:].rearrange("p (u m) -> p m u", u=PACK),
-            in_=w2s_plane[:].rearrange("p (m u) -> p m u", u=PACK),
+            out=w2_codes[:].bitcast(U16).rearrange("p (u m) -> p u m", u=PACK),
+            in_=w2_raw[:].bitcast(U16).rearrange("p (m u) -> p u m", u=PACK),
         )
         b_sb, b_banks = [], []
         for u in range(PACK):
@@ -168,22 +158,39 @@ def tile_picked_codes_refined_two_boardmeet_one_plain_kernel(
             copy_out(out=rows[:], in_=b_banks[u][:])
             b_sb.append(rows)
 
-        for u in range(2):
-            b_rows(u, nc.vector.tensor_copy, "b%d" % u)
 
-        for t in range(PACK):
-            wc_plane(t)
-        wc_grouped = new([P, R, PACK], BF16, "wc_grouped")
-        nc.vector.tensor_copy(
-            out=wc_grouped[:].bitcast(F32).rearrange("p (c i) g -> p c g i", i=RUN),
-            in_=wc_pairs[:].bitcast(F32).rearrange("p g (c i) one -> p c g (i one)", i=RUN),
-        )
+        def wc_terms(t):
+            coarse = new([P, R], F32, "coarse%d" % t)
+            fine = new([P, R], F32, "fine%d" % t)
+            nc.scalar.activation(out=coarse[:], in_=ua_sb[t][:].indirect(l2[:]), func=COPY, scale=ha_sb[:, t : t + 1])
+            nc.scalar.activation(out=fine[:], in_=ua_sb[t][:].indirect(l3[:]), func=COPY, scale=hb_sb[:, t : t + 1])
+            return coarse, fine
+
+        last = PACK - 1
+        wc_planes = new([P, last, R], BF16, "xs_plane")
+        for t in range(last):
+            coarse, fine = wc_terms(t)
+            nc.vector.tensor_tensor(out=wc_planes[:, t, :], in0=coarse[:], in1=fine[:], op=ADD)
+        wc_grouped = [new([P, 2 * P, PACK], BF16, "wc_grouped%d" % v) for v in range(2)]
+        for v in range(2):
+            nc.vector.tensor_copy(
+                out=wc_grouped[v][:, :, 0:last].rearrange("p (u c i) t -> p u c t i", u=2, i=2),
+                in_=wc_planes[:].rearrange("p t (c i v u) -> p v u c t i", i=2, v=2, u=2)[:, v],
+            )
+        coarse, fine = wc_terms(last)
+        for v in range(2):
+            nc.vector.tensor_tensor(
+                out=wc_grouped[v][:, :, last].rearrange("p (u m) -> p m u", u=2),
+                in0=coarse[:].rearrange("p (m v u) -> p v m u", v=2, u=2)[:, v],
+                in1=fine[:].rearrange("p (m v u) -> p v m u", v=2, u=2)[:, v],
+                op=ADD,
+            )
         wc_codes, wc_sc = [], []
 
         def wc_quantize(v, tag):
             codes = new([P, 2 * P], U32, tag)
             scales = new([P, 2 * P], U8, "wc_sc%d" % v)
-            quantize(codes[:], scales[:], wc_grouped[:, 2 * P * v : 2 * P * (v + 1), :])
+            quantize(codes[:], scales[:], wc_grouped[v][:])
             wc_codes.append(codes)
             wc_sc.append(scales)
 
@@ -233,7 +240,7 @@ def tile_picked_codes_refined_two_boardmeet_one_plain_kernel(
             a_piece(0, codes0[:, P * s : P * (s + 1)], sc0[:, P * s : P * (s + 1)], "a_bank%d" % s, "a0_0_%d" % s)
             for s in range(2)
         ]
-        rows0 = [a_piece(u, codes0[:], sc0[:], ("b_bank0", "b_bank1", "a_bank2")[u - 1], "a%d_0" % u) for u in range(1, PACK)]
+        rows0 = [a_piece(u, codes0[:], sc0[:], "a_bank%d" % ((u + 1) % PACK), "a%d_0" % u) for u in range(1, PACK)]
         for s in range(2):
             scatter(0, P * s, first[s])
         for u in range(1, PACK):
@@ -242,15 +249,15 @@ def tile_picked_codes_refined_two_boardmeet_one_plain_kernel(
         planes1 = xc_gather(1, "xc_codes0")
         grouped1 = new([P, HALF, PACK], BF16, "xc_grouped1")
         interleave(nc.scalar.copy, grouped1[:], planes1[:])
-        b_rows(2, nc.scalar.copy, "a1_0")
-        b_rows(3, nc.scalar.copy, "xc_codes0")
         codes1 = new([P, HALF], U32, "a2_0")
         sc1 = new([P, HALF], U8, "xc_sc1")
         quantize(codes1[:], sc1[:], grouped1[:])
-        rows1 = [a_piece(u, codes1[:], sc1[:], ("a_bank3", "a_bank0", "a_bank1", "a_bank2")[u], "a%d_1" % u) for u in range(PACK)]
+        rows1 = [a_piece(u, codes1[:], sc1[:], "a_bank%d" % ((u + 1) % PACK), "a%d_1" % u) for u in range(PACK)]
         for u in range(PACK):
             scatter(u, HALF, rows1[u])
 
+        for u, tag in enumerate(("xc_codes0", "xc_grouped1", "wc_codes0", "xc_sc1")):
+            b_rows(u, nc.scalar.copy, tag)
         from_board = new([P, PACK, O], F32, "from_board")
         from_b = new([P, PACK, O], F32, "a2_0")
         for u in range(PACK):
@@ -262,28 +269,33 @@ def tile_picked_codes_refined_two_boardmeet_one_plain_kernel(
                 out=from_board[:, u, :], in_=board[u][:].indirect(l6[:]), func=COPY, scale=sa_sb[:, u : u + 1]
             )
 
-        hid = new([P, O, PACK], BF16, "hid")
-        for rows in (slice(0, PACK - 1), slice(PACK - 1, PACK)):
+        def larger(hid, rows, cols):
             nc.vector.tensor_tensor(
-                out=hid[:, :, rows].rearrange("p (c i) t -> p c t i", i=RUN),
-                in0=from_board[:, rows, :].rearrange("p t (c i) -> p c t i", i=RUN),
-                in1=from_b[:, rows, :].rearrange("p t (c i) -> p c t i", i=RUN),
+                out=hid[:, :, rows].rearrange("p (c i) t -> p c t i", i=2),
+                in0=from_board[:, rows, cols].rearrange("p t (c i) -> p c t i", i=2),
+                in1=from_b[:, rows, cols].rearrange("p t (c i) -> p c t i", i=2),
                 op=MAX,
             )
-        hid_codes = new([P, O], U32, "hid_codes")
-        hid_sc = new([P, O], U8, "hid_sc")
-        quantize(hid_codes[:], hid_sc[:], hid[:])
-        for v, (copy_out, queue) in enumerate(((nc.vector.tensor_copy, nc.sync), (nc.scalar.copy, nc.scalar))):
-            bank = psum.tile([P, O], F32, name="b_bank%d" % v)
-            nc.tensor.matmul_mx(
-                out=bank[:],
-                lhsT=wb_sb[:, 2 * P * v : 2 * P * (v + 1)].bitcast(FP4X4),
-                lhsT_scale=wbs_plane[:, P * v : P * (v + 1)],
-                rhs=hid_codes[:].bitcast(FP8X4),
-                rhs_scale=hid_sc[:],
-                start=True,
-                stop=True,
-            )
-            result = new([P, O], F32, "result%d" % v)
+
+        hid = [new([P, P, PACK], BF16, "hid%d" % s) for s in range(2)]
+        for rows in (slice(0, PACK - 1), slice(PACK - 1, PACK)):
+            for s in range(2):
+                larger(hid[s], rows, slice(P * s, P * (s + 1)))
+        for s, (copy_out, queue) in enumerate(((nc.scalar.copy, nc.scalar), (nc.vector.tensor_copy, nc.sync))):
+            hid_codes = new([P, P], U32, "hid_codes%d" % s)
+            hid_sc = new([P, P], U8, "hid_sc%d" % s)
+            quantize(hid_codes[:], hid_sc[:], hid[s][:])
+            bank = psum.tile([P, 2, P], F32, name="b_bank%d" % s)
+            for v in range(2):
+                nc.tensor.matmul_mx(
+                    out=bank[:, v, :],
+                    lhsT=wb_sb[:, 2 * P * v : 2 * P * (v + 1)].bitcast(FP4X4),
+                    lhsT_scale=wbs_plane[:, P * v : P * (v + 1)],
+                    rhs=hid_codes[:].bitcast(FP8X4),
+                    rhs_scale=hid_sc[:],
+                    start=True,
+                    stop=True,
+                )
+            result = new([P, 2, P], F32, "result%d" % s)
             copy_out(out=result[:], in_=bank[:])
-            queue.dma_start(out[P * v : P * (v + 1), :], result[:])
+            queue.dma_start(out.rearrange("(v p) o -> p v o", v=2)[:, :, P * s : P * (s + 1)], result[:])

from contextlib import ExitStack

import concourse.mybir as mybir

K, J, R, T, F, Z, M, O, C, N = 512, 512, 512, 1024, 1024, 512, 1024, 256, 1024, 256
FLOPS = 2 * (K * R * J + Z * R * J + R * N * O)

F32 = mybir.dt.float32
BF16 = mybir.dt.bfloat16
I32 = mybir.dt.int32
U32 = mybir.dt.uint32
U16 = mybir.dt.uint16
U8 = mybir.dt.uint8
FP8X4 = mybir.dt.float8_e4m3fn_x4
FP4X4 = mybir.dt.float4_e2m1fn_x4
COPY = mybir.ActivationFunctionType.Copy
ADD = mybir.AluOpType.add
MAX = mybir.AluOpType.max

P = 128
PACK = 4
HALF = J // 2
STRIPE = 16
RUN = 4


def tile_picked_codes_refined_two_boardmeet_one_plain_kernel(
    tc, ta, ga, ua, ha, hb, xo_words, xo_scales, w2_words, w2_scales, sa, sb, wb_words, wb_scales,
    offs, offs2, offs3, offs4, offs5, offs6, offs7, out,
):
    nc = tc.nc
    with ExitStack() as ctx:
        keep = ctx.enter_context(tc.tile_pool(name="keep", bufs=1))
        psum = ctx.enter_context(tc.psum_pool(name="psum", bufs=1))

        def new(shape, dtype, name):
            return keep.tile(shape, dtype, name=name, align_bytes=64)

        def load_list(src, name):
            dst = keep.tile(list(src.shape), U16, name=name)
            nc.sync.dma_start(dst[:], src)
            return dst

        def load_factor(queue, src, name):
            dst = new([P, PACK], F32, name)
            queue.dma_start(dst[:], src.rearrange("(p t) one -> p (t one)", t=PACK))
            return dst

        def load_plane(src, t, name):
            dst = new([P, src.shape[1]], F32, name)
            nc.sync.dma_start(dst[:], src.rearrange("(p t) c -> p t c", t=PACK)[:, t, :])
            return dst

        def load_words(src, dtype, width, name):
            dst = new([P, width], dtype, name)
            nc.sync.dma_start(dst[:].bitcast(I32), src.bitcast(I32))
            return dst

        def load_scale_rows(src, name):
            width = src.shape[2]
            stage = new([4, 4, width // 4], I32, name)
            nc.sync.dma_start(stage[:], src[0].bitcast(I32).rearrange("(q i) w -> i q w", i=4))
            return stage

        def zeroed_plane(engine, width, name):
            plane = new([P, width], U8, name)
            engine.memset(plane[:].bitcast(I32), 0)
            return plane

        def spread(plane, stage):
            for q in range(4):
                nc.vector.tensor_copy(out=plane[32 * q : 32 * q + 4, :].bitcast(I32), in_=stage[:, q, :])

        def interleave(engine_copy, dst, src):
            engine_copy(
                out=dst.rearrange("p (c i) t -> p c t i", i=RUN),
                in_=src.rearrange("p t (c i) -> p c t i", i=RUN),
            )

        def quantize(codes, scales, grouped):
            nc.vector.quantize_mx(out=codes.bitcast(FP8X4), scales=scales, in_=grouped.rearrange("p c t -> p (c t)"))

        xs_plane = zeroed_plane(nc.gpsimd, M, "xs_plane")
        w2s_plane = zeroed_plane(nc.vector, R, "w2s_plane")
        wbs_plane = zeroed_plane(nc.vector, N, "wbs_plane")

        def load_scales_in_place(plane, src):
            for q in range(4):
                nc.sync.dma_start(
                    plane[32 * q : 32 * q + 4, :].bitcast(I32), src[0, 4 * q : 4 * q + 4, :].bitcast(I32)
                )

        l2 = load_list(offs2, "l2")
        ha_sb = load_factor(nc.scalar, ha, "ha_sb")
        hb_sb = load_factor(nc.scalar, hb, "hb_sb")
        ua_sb = [load_plane(ua, 0, "ua0")]
        l3 = load_list(offs3, "l3")
        w2s_stage = load_scale_rows(w2_scales, "w2s_stage")
        ua_sb.append(load_plane(ua, 1, "ua1"))
        l4 = load_list(offs4, "l4")
        xo_sb = load_words(xo_words[0].rearrange("p c t -> p (c t)"), U32, M, "xo_sb")
        load_scales_in_place(xs_plane, xo_scales)
        w2_raw = load_words(w2_words[0], U8, 2 * R, "w2_raw")
        ua_sb.append(load_plane(ua, 2, "ua2"))
        ua_sb.append(load_plane(ua, 3, "ua3"))
        l1 = load_list(offs, "l1")
        ga_sb = load_factor(nc.sync, ga, "ga_sb")
        ta_sb = [load_plane(ta, t, "ta%d" % t) for t in range(PACK)]
        l5 = load_list(offs5, "l5")
        l7 = load_list(offs7, "l7")
        sb_sb = load_factor(nc.sync, sb, "sb_sb")
        l6 = load_list(offs6, "l6")
        sa_sb = load_factor(nc.sync, sa, "sa_sb")
        wb_sb = load_words(wb_words[0], U8, 2 * N, "wb_sb")

        load_scales_in_place(wbs_plane, wb_scales)

        warm_in = new([P, 1], F32, "warm_in")
        warm_out = new([P, 1], F32, "warm_out")
        nc.gpsimd.memset(warm_in[:], 0.0)
        nc.scalar.activation(out=warm_out[:], in_=warm_in[:], func=COPY)

        board = [new([P, C], F32, "board%d" % t) for t in range(PACK)]
        for t in range(PACK):
            (nc.vector if t < 2 else nc.gpsimd).memset(board[t][:], 0.0)

        spread(w2s_plane, w2s_stage)
        w2_codes = new([P, 2 * R], U8, "w2_codes")
        w2_sc = new([P, R], U8, "w2_sc")
        nc.vector.tensor_copy(
            out=w2_sc[:].rearrange("p (u m) -> p u m", u=PACK),
            in_=w2s_plane[:].rearrange("p (m u) -> p u m", u=PACK),
        )
        note_codes = new([P, J], U32, "note_codes")
        note_sc = new([P, J], U8, "note_sc")
        nc.vector.tensor_copy(out=note_codes[:], in_=xo_sb[:].indirect(l4[:]))
        nc.vector.tensor_copy(out=note_sc[:], in_=xs_plane[:].indirect(l4[:]))
        nc.vector.tensor_copy(
            out=w2_codes[:].bitcast(U16).rearrange("p (u m) -> p u m", u=PACK),
            in_=w2_raw[:].bitcast(U16).rearrange("p (m u) -> p u m", u=PACK),
        )
        b_sb, b_banks = [], []
        for u in range(PACK):
            bank = psum.tile([P, J], F32, name="b_bank%d" % u)
            nc.tensor.matmul_mx(
                out=bank[:],
                lhsT=w2_codes[:, 2 * P * u : 2 * P * (u + 1)].bitcast(FP4X4),
                lhsT_scale=w2_sc[:, P * u : P * (u + 1)],
                rhs=note_codes[:].bitcast(FP8X4),
                rhs_scale=note_sc[:],
                start=True,
                stop=True,
            )
            b_banks.append(bank)

        def b_rows(u, copy_out, tag):
            rows = new([P, J], F32, tag)
            copy_out(out=rows[:], in_=b_banks[u][:])
            b_sb.append(rows)


        def wc_terms(t):
            coarse = new([P, R], F32, "coarse%d" % t)
            fine = new([P, R], F32, "fine%d" % t)
            nc.scalar.activation(out=coarse[:], in_=ua_sb[t][:].indirect(l2[:]), func=COPY, scale=ha_sb[:, t : t + 1])
            nc.scalar.activation(out=fine[:], in_=ua_sb[t][:].indirect(l3[:]), func=COPY, scale=hb_sb[:, t : t + 1])
            return coarse, fine

        last = PACK - 1
        wc_planes = new([P, last, R], BF16, "xs_plane")
        for t in range(last):
            coarse, fine = wc_terms(t)
            nc.vector.tensor_tensor(out=wc_planes[:, t, :], in0=coarse[:], in1=fine[:], op=ADD)
        wc_grouped = [new([P, 2 * P, PACK], BF16, "wc_grouped%d" % v) for v in range(2)]
        for v in range(2):
            nc.vector.tensor_copy(
                out=wc_grouped[v][:, :, 0:last].rearrange("p (u c i) t -> p u c t i", u=2, i=2),
                in_=wc_planes[:].rearrange("p t (c i v u) -> p v u c t i", i=2, v=2, u=2)[:, v],
            )
        coarse, fine = wc_terms(last)
        for v in range(2):
            nc.vector.tensor_tensor(
                out=wc_grouped[v][:, :, last].rearrange("p (u m) -> p m u", u=2),
                in0=coarse[:].rearrange("p (m v u) -> p v m u", v=2, u=2)[:, v],
                in1=fine[:].rearrange("p (m v u) -> p v m u", v=2, u=2)[:, v],
                op=ADD,
            )
        wc_codes, wc_sc = [], []

        def wc_quantize(v, tag):
            codes = new([P, 2 * P], U32, tag)
            scales = new([P, 2 * P], U8, "wc_sc%d" % v)
            quantize(codes[:], scales[:], wc_grouped[v][:])
            wc_codes.append(codes)
            wc_sc.append(scales)

        wc_quantize(0, "wc_codes0")

        def xc_gather(h, tag):
            planes = new([P, PACK, HALF], BF16, tag)
            cols = slice(h * HALF // STRIPE, (h + 1) * HALF // STRIPE)
            for t in range(PACK):
                nc.scalar.activation(
                    out=planes[:, t, :], in_=ta_sb[t][:].indirect(l1[:, cols]), func=COPY, scale=ga_sb[:, t : t + 1]
                )
            return planes

        def a_piece(u, codes, scales, bank_tag, rows_tag):
            width = codes.shape[1]
            bank = psum.tile([P, width], F32, name=bank_tag)
            nc.tensor.matmul_mx(
                out=bank[:],
                lhsT=wc_codes[u // 2][:, P * (u % 2) : P * (u % 2 + 1)].bitcast(FP8X4),
                lhsT_scale=wc_sc[u // 2][:, P * (u % 2) : P * (u % 2 + 1)],
                rhs=codes.bitcast(FP8X4),
                rhs_scale=scales,
                start=True,
                stop=True,
            )
            rows = new([P, width], F32, rows_tag)
            nc.scalar.copy(out=rows[:], in_=bank[:])
            return rows

        def scatter(u, first, rows):
            width = rows.shape[1]
            nc.vector.tensor_copy(
                out=board[u][:].indirect(l5[:, first // STRIPE : (first + width) // STRIPE]), in_=rows[:]
            )

        planes0 = xc_gather(0, "xc_planes0")
        grouped0 = [new([P, P, PACK], BF16, "xc_grouped0_%d" % s) for s in range(2)]
        codes0 = new([P, HALF], U32, "xc_codes0")
        sc0 = new([P, HALF], U8, "xc_sc0")
        for s in range(2):
            interleave(nc.vector.tensor_copy, grouped0[s][:], planes0[:, :, P * s : P * (s + 1)])
        for s in range(2):
            quantize(codes0[:, P * s : P * (s + 1)], sc0[:, P * s : P * (s + 1)], grouped0[s][:])
        wc_quantize(1, "xc_planes0")
        first = [
            a_piece(0, codes0[:, P * s : P * (s + 1)], sc0[:, P * s : P * (s + 1)], "a_bank%d" % s, "a0_0_%d" % s)
            for s in range(2)
        ]
        rows0 = [a_piece(u, codes0[:], sc0[:], "a_bank%d" % ((u + 1) % PACK), "a%d_0" % u) for u in range(1, PACK)]
        for s in range(2):
            scatter(0, P * s, first[s])
        for u in range(1, PACK):
            scatter(u, 0, rows0[u - 1])

        planes1 = xc_gather(1, "xc_codes0")
        grouped1 = new([P, HALF, PACK], BF16, "xc_grouped1")
        interleave(nc.scalar.copy, grouped1[:], planes1[:])
        codes1 = new([P, HALF], U32, "a2_0")
        sc1 = new([P, HALF], U8, "xc_sc1")
        quantize(codes1[:], sc1[:], grouped1[:])
        rows1 = [a_piece(u, codes1[:], sc1[:], "a_bank%d" % ((u + 1) % PACK), "a%d_1" % u) for u in range(PACK)]
        for u in range(PACK):
            scatter(u, HALF, rows1[u])

        for u, tag in enumerate(("xc_codes0", "xc_grouped1", "wc_codes0", "xc_sc1")):
            b_rows(u, nc.scalar.copy, tag)
        from_board = new([P, PACK, O], F32, "from_board")
        from_b = new([P, PACK, O], F32, "a2_0")
        for u in range(PACK):
            nc.scalar.activation(
                out=from_b[:, u, :], in_=b_sb[u][:].indirect(l7[:]), func=COPY, scale=sb_sb[:, u : u + 1]
            )
        for u in range(PACK):
            nc.scalar.activation(
                out=from_board[:, u, :], in_=board[u][:].indirect(l6[:]), func=COPY, scale=sa_sb[:, u : u + 1]
            )

        def larger(hid, rows, cols):
            nc.vector.tensor_tensor(
                out=hid[:, :, rows].rearrange("p (c i) t -> p c t i", i=2),
                in0=from_board[:, rows, cols].rearrange("p t (c i) -> p c t i", i=2),
                in1=from_b[:, rows, cols].rearrange("p t (c i) -> p c t i", i=2),
                op=MAX,
            )

        hid = [new([P, P, PACK], BF16, "hid%d" % s) for s in range(2)]
        for rows in (slice(0, PACK - 1), slice(PACK - 1, PACK)):
            for s in range(2):
                larger(hid[s], rows, slice(P * s, P * (s + 1)))
        for s, (copy_out, queue) in enumerate(((nc.scalar.copy, nc.scalar), (nc.vector.tensor_copy, nc.sync))):
            hid_codes = new([P, P], U32, "hid_codes%d" % s)
            hid_sc = new([P, P], U8, "hid_sc%d" % s)
            quantize(hid_codes[:], hid_sc[:], hid[s][:])
            bank = psum.tile([P, 2, P], F32, name="b_bank%d" % s)
            for v in range(2):
                nc.tensor.matmul_mx(
                    out=bank[:, v, :],
                    lhsT=wb_sb[:, 2 * P * v : 2 * P * (v + 1)].bitcast(FP4X4),
                    lhsT_scale=wbs_plane[:, P * v : P * (v + 1)],
                    rhs=hid_codes[:].bitcast(FP8X4),
                    rhs_scale=hid_sc[:],
                    start=True,
                    stop=True,
                )
            result = new([P, 2, P], F32, "result%d" % s)
            copy_out(out=result[:], in_=bank[:])
            queue.dma_start(out.rearrange("(v p) o -> p v o", v=2)[:, :, P * s : P * (s + 1)], result[:])
